import numpy as np
import ml_dtypes


def mxq(x, axis, fmt="e4m3"):
    dtype, down = {"e4m3": (ml_dtypes.float8_e4m3fn, 7), "e5m2": (ml_dtypes.float8_e5m2, 14)}[fmt]
    v = np.moveaxis(np.asarray(x, np.float32).astype(ml_dtypes.bfloat16).astype(np.float64), axis, -1)
    blocks = v.reshape(v.shape[:-1] + (-1, 32))
    amax = np.abs(blocks).max(-1, keepdims=True)
    byte = np.maximum(np.where(amax > 0, np.frexp(amax)[1] - 1 + 127, 0) - down, 1)
    scale = np.exp2(byte - 127.0)
    codes = (blocks / scale).astype(np.float32).astype(dtype).astype(np.float64)
    return np.moveaxis((codes * scale).reshape(v.shape), -1, axis)


WIDE = False


def mx_kscale(k):
    if not WIDE:
        return np.ones(k)
    levels = np.array([10, -10, 5, -5, 0])
    if k % 512:
        return np.exp2(np.random.permutation(np.resize(levels, k // 32))).repeat(32)
    a = np.empty((k // 512, 16))
    for p in range(k // 512):
        a[p, :8] = np.random.permutation(np.resize(levels, 8))
        for g in range(8):
            far = levels[np.abs(levels - a[p, g]) >= 10]
            a[p, g + 8] = far[np.random.randint(len(far))]
    return np.exp2(a.ravel()).repeat(32)


def f64(x):
    return np.asarray(x).astype(np.float64)


def striped(idx):
    return np.tile(idx.reshape(-1, 16).T, (8, 1)).astype(np.uint16)


def unstriped(offs):
    return offs[:16].T.reshape(-1).astype(np.int64)


def relu2(v):
    return np.maximum(v, 0.0) ** 2


K, T, S, H, N = 1536, 1024, 512, 1024, 512


def setup_inputs():
    n = np.random.standard_normal
    s = mx_kscale(K)[:, None]
    u = mx_kscale(H)
    return {
        "xT": (n((K, S)) * s).astype(np.float32),
        "w1": (n((K, H)) / np.sqrt(K) / s * u).astype(np.float32),
        "w2": (n((H, N)) / np.sqrt(H) / u[:, None] ** 2).astype(np.float32),
        "gate": np.tile(np.random.uniform(0.2, 1.0, S), (N, 1)).astype(np.float32),
        "offs": striped(np.sort(np.random.permutation(T)[:S])),
    }


def reference(xT, w1, w2, gate, offs):
    idx = unstriped(offs)
    xq = mxq(f64(xT), 0, "e4m3")
    h = relu2(mxq(f64(w1), 0, "e4m3").T @ xq)
    y = mxq(f64(w2), 0, "e4m3").T @ mxq(h, 0, "e4m3")
    out = np.zeros((N, T))
    out[:, idx] = f64(gate) * y
    return out

@@ -1,0 +1,143 @@
+from contextlib import ExitStack
+
+import concourse.mybir as mybir
+
+K, T, S, H, N = 1536, 1024, 512, 1024, 512
+FLOPS = 2 * S * H * (K + N)
+
+F32 = mybir.dt.float32
+BF16 = mybir.dt.bfloat16
+U32 = mybir.dt.uint32
+U16 = mybir.dt.uint16
+U8 = mybir.dt.uint8
+FP8X4 = mybir.dt.float8_e4m3fn_x4
+MULT = mybir.AluOpType.mult
+RELU = mybir.ActivationFunctionType.Relu
+SQUARE = mybir.ActivationFunctionType.Square
+
+P = 128
+PASS = 512
+HALF = 512
+V_COLS = 256
+V_M = 64
+
+
+def tile_picked_place_mlp_relu2_srt_l_kernel(tc, xT, w1, w2, gate, offs, out):
+    nc = tc.nc
+    passes = K // PASS
+    with ExitStack() as ctx:
+        keep = ctx.enter_context(tc.tile_pool(name="keep", bufs=1))
+        psum = ctx.enter_context(tc.psum_pool(name="psum", bufs=8))
+
+        def raw_tile(name):
+            return keep.tile([P, 4, 512], F32, name=name)
+
+        def load(tile, rows):
+            nc.sync.dma_start(out=tile[:], in_=rows.rearrange("(p j) w -> p j w", j=4))
+
+        offsets = keep.tile([P, S // 16], U16, name="offsets")
+        gates = keep.tile([P, 4, S], F32, name="gates")
+        x_raw = [raw_tile("x_raw%d" % c) for c in range(passes)]
+        w1_raw = [[raw_tile("w1_raw%d%d" % (h, c)) for c in range(passes)] for h in range(2)]
+        w2_raw = [raw_tile("w2_raw%d" % h) for h in range(2)]
+        windows = [keep.tile([P, T], F32, name="window%d" % b) for b in range(4)]
+
+        for c in range(passes):
+            load(x_raw[c], xT[c * PASS : (c + 1) * PASS, :])
+            load(w1_raw[0][c], w1[c * PASS : (c + 1) * PASS, 0:HALF])
+        load(w1_raw[1][0], w1[0:PASS, HALF:])
+        load(w1_raw[1][1], w1[PASS : 2 * PASS, HALF:])
+        load(w2_raw[0], w2[0:HALF, :])
+        load(w1_raw[1][2], w1[2 * PASS : 3 * PASS, HALF:])
+        load(w2_raw[1], w2[HALF:, :])
+        nc.sync.dma_start(offsets[:], offs)
+        nc.sync.dma_start(out=gates[:], in_=gate.rearrange("(b p) n -> p b n", p=P))
+
+        for b in range(4):
+            nc.vector.memset(windows[b][:], 0.0)
+
+        def quantize(grouped, name):
+            codes = keep.tile([P, 512], U32, name=name + "_codes", align_bytes=64)
+            scales = keep.tile([P, 512], U8, name=name + "_scales", align_bytes=64)
+            nc.vector.quantize_mx(out=codes[:].bitcast(FP8X4), scales=scales[:], in_=grouped)
+            return codes, scales
+
+        def plain_chunk(raw, name):
+            grouped = keep.tile([P, 512, 4], BF16, name=name + "_grouped", align_bytes=64)
+            for engine_copy, lo, hi in ((nc.vector.tensor_copy, 0, V_COLS), (nc.scalar.copy, V_COLS, 512)):
+                engine_copy(
+                    out=grouped[:, lo:hi, :].rearrange("p (c i) j -> p c j i", i=4),
+                    in_=raw[:, :, lo:hi].rearrange("p j (c i) -> p c j i", i=4),
+                )
+            return quantize(grouped[:].rearrange("p w j -> p (w j)"), name)
+
+        def permuted_chunk(raw, name):
+            grouped = keep.tile([P, 4, P, 4], BF16, name=name + "_grouped", align_bytes=64)
+            for engine_copy, lo, hi in ((nc.vector.tensor_copy, 0, V_M), (nc.scalar.copy, V_M, P)):
+                engine_copy(
+                    out=grouped[:, :, lo:hi, :].rearrange("p t m j -> p m j t"),
+                    in_=raw[:, :, 4 * lo : 4 * hi].rearrange("p j (m t) -> p m j t", t=4),
+                )
+            return quantize(grouped[:].rearrange("p t m j -> p (t m j)"), name)
+
+        def multiply(acc, stationary, tile_index, moving, first, last):
+            cols = slice(tile_index * P, (tile_index + 1) * P)
+            nc.tensor.matmul_mx(
+                out=acc[:],
+                lhsT=stationary[0][:, cols].bitcast(FP8X4),
+                lhsT_scale=stationary[1][:, cols],
+                rhs=moving[0][:].bitcast(FP8X4),
+                rhs_scale=moving[1][:],
+                start=first,
+                stop=last,
+            )
+
+        def relu2(acc, name):
+            positive = keep.tile([P, 4, S], F32, name=name + "_positive")
+            for t in range(4):
+                if t % 2 == 0:
+                    nc.scalar.activation(positive[:, t, :], acc[t][:], RELU)
+                else:
+                    nc.vector.tensor_scalar_max(positive[:, t, :], acc[t][:], 0.0)
+            grouped = keep.tile([P, S, 4], BF16, name=name + "_grouped", align_bytes=64)
+
+            def views(lo, hi):
+                return (
+                    grouped[:, lo:hi, :].rearrange("p (c i) t -> p c t i", i=4),
+                    positive[:, :, lo:hi].rearrange("p t (c i) -> p c t i", i=4),
+                )
+
+            dst, src = views(0, V_COLS)
+            nc.vector.tensor_tensor(dst, src, src, MULT)
+            dst, src = views(V_COLS, S)
+            nc.scalar.activation(dst, src, SQUARE)
+            return quantize(grouped[:].rearrange("p w t -> p (w t)"), name)
+
+        x_q = []
+        acc = [psum.tile([P, S], F32, name="bank") for t in range(4)]
+        for c in range(passes):
+            x_q.append(plain_chunk(x_raw[c], "x%d" % c))
+            w1_q = permuted_chunk(w1_raw[0][c], "w1a%d" % c)
+            for t in range(4):
+                multiply(acc[t], w1_q, t, x_q[c], c == 0, c == passes - 1)
+        h_q = [relu2(acc, "ha")]
+
+        acc = [psum.tile([P, S], F32, name="bank") for t in range(4)]
+        w2_q = []
+        for c in range(passes):
+            if c == passes - 1:
+                w2_q.append(plain_chunk(w2_raw[0], "w2a"))
+            w1_q = permuted_chunk(w1_raw[1][c], "w1b%d" % c)
+            for t in range(4):
+                multiply(acc[t], w1_q, t, x_q[c], c == 0, c == passes - 1)
+        y = [psum.tile([P, S], F32, name="bank") for b in range(4)]
+        for b in range(4):
+            multiply(y[b], w2_q[0], b, h_q[0], True, False)
+        h_q.append(relu2(acc, "hb"))
+        w2_q.append(plain_chunk(w2_raw[1], "w2b"))
+        for b in range(4):
+            multiply(y[b], w2_q[1], b, h_q[1], False, True)
+            results = keep.tile([P, S], F32, name="results%d" % b)
+            nc.scalar.copy(results[:], y[b][:])
+            nc.vector.tensor_tensor(windows[b][:].indirect(offsets[:]), results[:], gates[:, b, :], MULT)
+            nc.sync.dma_start(out=out[b * P : (b + 1) * P, :], in_=windows[b][:])

@@ -18,126 +18,192 @@ SQUARE = mybir.ActivationFunctionType.Square
 P = 128
 PASS = 512
 HALF = 512
-V_COLS = 256
-V_M = 64
 
 
 def tile_picked_place_mlp_relu2_srt_l_kernel(tc, xT, w1, w2, gate, offs, out):
     nc = tc.nc
-    passes = K // PASS
     with ExitStack() as ctx:
         keep = ctx.enter_context(tc.tile_pool(name="keep", bufs=1))
         psum = ctx.enter_context(tc.psum_pool(name="psum", bufs=8))
 
-        def raw_tile(name):
-            return keep.tile([P, 4, 512], F32, name=name)
-
-        def load(tile, rows):
-            nc.sync.dma_start(out=tile[:], in_=rows.rearrange("(p j) w -> p j w", j=4))
-
         offsets = keep.tile([P, S // 16], U16, name="offsets")
-        gates = keep.tile([P, 4, S], F32, name="gates")
-        x_raw = [raw_tile("x_raw%d" % c) for c in range(passes)]
-        w1_raw = [[raw_tile("w1_raw%d%d" % (h, c)) for c in range(passes)] for h in range(2)]
-        w2_raw = [raw_tile("w2_raw%d" % h) for h in range(2)]
+        gates = [keep.tile([P, S], F32, name="gate%d" % b) for b in range(4)]
         windows = [keep.tile([P, T], F32, name="window%d" % b) for b in range(4)]
+        raw = {}
 
-        for c in range(passes):
-            load(x_raw[c], xT[c * PASS : (c + 1) * PASS, :])
-            load(w1_raw[0][c], w1[c * PASS : (c + 1) * PASS, 0:HALF])
-        load(w1_raw[1][0], w1[0:PASS, HALF:])
-        load(w1_raw[1][1], w1[PASS : 2 * PASS, HALF:])
-        load(w2_raw[0], w2[0:HALF, :])
-        load(w1_raw[1][2], w1[2 * PASS : 3 * PASS, HALF:])
-        load(w2_raw[1], w2[HALF:, :])
+        def load(name, rows):
+            raw[name] = keep.tile([P, 4, rows.shape[1]], F32, name=name + "_raw")
+            nc.sync.dma_start(out=raw[name][:], in_=rows.rearrange("(p j) w -> p j w", j=4))
+
+        load("x0", xT[0:512, :])
+        load("w0", w1[0:512, :])
+        load("x1", xT[512:1024, :])
+        load("a1", w1[512:1024, 0:512])
+        load("x2", xT[1024:1536, :])
+        load("a2", w1[1024:1536, 0:512])
+        load("b1", w1[512:1024, 512:1024])
+        load("b2", w1[1024:1536, 512:1024])
+        load("u0", w2[0:512, :])
+        load("u1", w2[512:1024, :])
         nc.sync.dma_start(offsets[:], offs)
-        nc.sync.dma_start(out=gates[:], in_=gate.rearrange("(b p) n -> p b n", p=P))
-
+        for b in range(4):
+            nc.sync.dma_start(out=gates[b][:], in_=gate[b * P : (b + 1) * P, :])
         for b in range(4):
             nc.vector.memset(windows[b][:], 0.0)
 
-        def quantize(grouped, name):
-            codes = keep.tile([P, 512], U32, name=name + "_codes", align_bytes=64)
-            scales = keep.tile([P, 512], U8, name=name + "_scales", align_bytes=64)
-            nc.vector.quantize_mx(out=codes[:].bitcast(FP8X4), scales=scales[:], in_=grouped)
-            return codes, scales
+        grouped = {}
+        codes = {}
 
-        def plain_chunk(raw, name):
-            grouped = keep.tile([P, 512, 4], BF16, name=name + "_grouped", align_bytes=64)
-            for engine_copy, lo, hi in ((nc.vector.tensor_copy, 0, V_COLS), (nc.scalar.copy, V_COLS, 512)):
+        def shares(v, total):
+            return [s for s in ((nc.vector.tensor_copy, 0, v), (nc.scalar.copy, v, total)) if s[1] < s[2]]
+
+        def copy_plain(name, pieces):
+            src = raw[name]
+            if name not in grouped:
+                grouped[name] = keep.tile([P, 512, 4], BF16, name=name + "_grouped", align_bytes=64)
+            for engine_copy, lo, hi in pieces:
                 engine_copy(
-                    out=grouped[:, lo:hi, :].rearrange("p (c i) j -> p c j i", i=4),
-                    in_=raw[:, :, lo:hi].rearrange("p j (c i) -> p c j i", i=4),
+                    out=grouped[name][:, lo:hi, :].rearrange("p (c i) j -> p c j i", i=4),
+                    in_=src[:, :, lo:hi].rearrange("p j (c i) -> p c j i", i=4),
                 )
-            return quantize(grouped[:].rearrange("p w j -> p (w j)"), name)
 
-        def permuted_chunk(raw, name):
-            grouped = keep.tile([P, 4, P, 4], BF16, name=name + "_grouped", align_bytes=64)
-            for engine_copy, lo, hi in ((nc.vector.tensor_copy, 0, V_M), (nc.scalar.copy, V_M, P)):
+        def copy_permuted(name, src, v):
+            grouped[name] = keep.tile([P, 4, P, 4], BF16, name=name + "_grouped", align_bytes=64)
+            for engine_copy, lo, hi in shares(v, P):
                 engine_copy(
-                    out=grouped[:, :, lo:hi, :].rearrange("p t m j -> p m j t"),
-                    in_=raw[:, :, 4 * lo : 4 * hi].rearrange("p j (m t) -> p m j t", t=4),
+                    out=grouped[name][:, :, lo:hi, :].rearrange("p t m j -> p m j t"),
+                    in_=src[:, :, 4 * lo : 4 * hi].rearrange("p j (m t) -> p m j t", t=4),
                 )
-            return quantize(grouped[:].rearrange("p t m j -> p (t m j)"), name)
 
-        def multiply(acc, stationary, tile_index, moving, first, last):
-            cols = slice(tile_index * P, (tile_index + 1) * P)
+        def quantize(name, parts=((0, 512),)):
+            src = grouped[name]
+            flat = src[:].rearrange("p t m j -> p (t m j)") if len(src.shape) == 4 else src[:].rearrange("p w j -> p (w j)")
+            if name not in codes:
+                codes[name] = (
+                    keep.tile([P, 512], U32, name=name + "_codes", align_bytes=64),
+                    keep.tile([P, 512], U8, name=name + "_scales", align_bytes=64),
+                )
+            words, scales = codes[name]
+            for lo, hi in parts:
+                nc.vector.quantize_mx(out=words[:, lo:hi].bitcast(FP8X4), scales=scales[:, lo:hi], in_=flat[:, 4 * lo : 4 * hi])
+
+        QUARTERS = [(128 * t, 128 * t + 128) for t in range(4)]
+
+        def multiply(acc, weights, t, tokens, moving, first, last):
+            cols = slice(t * P, (t + 1) * P)
             nc.tensor.matmul_mx(
                 out=acc[:],
-                lhsT=stationary[0][:, cols].bitcast(FP8X4),
-                lhsT_scale=stationary[1][:, cols],
-                rhs=moving[0][:].bitcast(FP8X4),
-                rhs_scale=moving[1][:],
+                lhsT=codes[weights][0][:, cols].bitcast(FP8X4),
+                lhsT_scale=codes[weights][1][:, cols],
+                rhs=codes[moving][0][:, tokens].bitcast(FP8X4),
+                rhs_scale=codes[moving][1][:, tokens],
                 start=first,
                 stop=last,
             )
 
-        def relu2(acc, name):
-            positive = keep.tile([P, 4, S], F32, name=name + "_positive")
+        ALL = slice(0, S)
+        acc = {}
+
+        def layer1(half, c):
+            if c == 0:
+                acc[half] = [psum.tile([P, S], F32, name="bank") for t in range(4)]
             for t in range(4):
-                if t % 2 == 0:
-                    nc.scalar.activation(positive[:, t, :], acc[t][:], RELU)
+                multiply(acc[half][t], "%s%d" % (half, c), t, ALL, "x%d" % c, c == 0, c == 2)
+
+        positive = {}
+
+        def relu(half, engines):
+            positive[half] = keep.tile([P, 4, S], F32, name=half + "_positive")
+            for t in range(4):
+                if engines[t] == "S":
+                    nc.scalar.activation(positive[half][:, t, :], acc[half][t][:], RELU)
                 else:
-                    nc.vector.tensor_scalar_max(positive[:, t, :], acc[t][:], 0.0)
-            grouped = keep.tile([P, S, 4], BF16, name=name + "_grouped", align_bytes=64)
+                    nc.vector.tensor_scalar_max(positive[half][:, t, :], acc[half][t][:], 0.0)
 
-            def views(lo, hi):
-                return (
-                    grouped[:, lo:hi, :].rearrange("p (c i) t -> p c t i", i=4),
-                    positive[:, :, lo:hi].rearrange("p t (c i) -> p c t i", i=4),
-                )
+        def square(half, lo, mid, hi):
+            name = "h" + half
+            if name not in grouped:
+                grouped[name] = keep.tile([P, S, 4], BF16, name=name + "_grouped", align_bytes=64)
+            for on_scalar, a, b in ((False, lo, mid), (True, mid, hi)):
+                if a == b:
+                    continue
+                dst = grouped[name][:, a:b, :].rearrange("p (c i) t -> p c t i", i=4)
+                src = positive[half][:, :, a:b].rearrange("p t (c i) -> p c t i", i=4)
+                if on_scalar:
+                    nc.scalar.activation(dst, src, SQUARE)
+                else:
+                    nc.vector.tensor_tensor(dst, src, src, MULT)
 
-            dst, src = views(0, V_COLS)
-            nc.vector.tensor_tensor(dst, src, src, MULT)
-            dst, src = views(V_COLS, S)
-            nc.scalar.activation(dst, src, SQUARE)
-            return quantize(grouped[:].rearrange("p w t -> p (w t)"), name)
+        VC, SC = nc.vector.tensor_copy, nc.scalar.copy
+        EVEN = ((VC, 0, 256), (SC, 256, 512))
+        copy_plain("x0", EVEN)
+        copy_permuted("a0", raw["w0"][:, :, 0:512], 80)
+        quantize("x0")
+        copy_permuted("b0", raw["w0"][:, :, 512:1024], 64)
+        quantize("a0")
+        layer1("a", 0)
+        quantize("b0")
+        copy_plain("x1", EVEN)
+        quantize("x1")
+        copy_permuted("a1", raw["a1"], 80)
+        quantize("a1")
+        layer1("a", 1)
+        copy_plain("x2", EVEN)
+        quantize("x2")
+        copy_permuted("a2", raw["a2"], 80)
+        quantize("a2", QUARTERS)
+        layer1("a", 2)
+        relu("a", "SVSV")
+        copy_permuted("b1", raw["b1"], 96)
+        square("a", 0, 192, 512)
+        quantize("b1")
+        layer1("b", 0)
+        layer1("b", 1)
+        quantize("ha")
+        copy_permuted("b2", raw["b2"], 88)
+        quantize("b2", QUARTERS)
+        layer1("b", 2)
+        copy_plain("u0", ((VC, 0, 256),))
+        relu("b", "SVSV")
+        quantize("u0", ((0, 256),))
+        FIRST, SECOND = slice(0, 256), slice(256, 512)
+        ya = [psum.tile([P, 256], F32, name="bank") for b in range(4)]
+        for b in range(2):
+            multiply(ya[b], "u0", b, FIRST, "ha", True, False)
+        square("b", 0, 128, 256)
+        quantize("hb", ((0, 256),))
+        square("b", 256, 256, 512)
+        copy_plain("u1", ((VC, 0, 256),))
+        quantize("u1", ((0, 256),))
+        for b in range(2):
+            multiply(ya[b], "u1", b, FIRST, "hb", False, True)
+        quantize("hb", ((256, 512),))
+        yb = [psum.tile([P, 256], F32, name="bank") for b in range(4)]
+        results = [keep.tile([P, S], F32, name="results%d" % b) for b in range(4)]
 
-        x_q = []
-        acc = [psum.tile([P, S], F32, name="bank") for t in range(4)]
-        for c in range(passes):
-            x_q.append(plain_chunk(x_raw[c], "x%d" % c))
-            w1_q = permuted_chunk(w1_raw[0][c], "w1a%d" % c)
-            for t in range(4):
-                multiply(acc[t], w1_q, t, x_q[c], c == 0, c == passes - 1)
-        h_q = [relu2(acc, "ha")]
+        def finish(b, y, tokens):
+            lo, hi = tokens.start, tokens.stop
+            nc.scalar.copy(results[b][:, lo:hi], y[b][:])
+            nc.vector.tensor_tensor(
+                windows[b][:].indirect(offsets[:, lo // 16 : hi // 16]), results[b][:, lo:hi], gates[b][:, lo:hi], MULT
+            )
 
-        acc = [psum.tile([P, S], F32, name="bank") for t in range(4)]
-        w2_q = []
-        for c in range(passes):
-            if c == passes - 1:
-                w2_q.append(plain_chunk(w2_raw[0], "w2a"))
-            w1_q = permuted_chunk(w1_raw[1][c], "w1b%d" % c)
-            for t in range(4):
-                multiply(acc[t], w1_q, t, x_q[c], c == 0, c == passes - 1)
-        y = [psum.tile([P, S], F32, name="bank") for b in range(4)]
-        for b in range(4):
-            multiply(y[b], w2_q[0], b, h_q[0], True, False)
-        h_q.append(relu2(acc, "hb"))
-        w2_q.append(plain_chunk(w2_raw[1], "w2b"))
-        for b in range(4):
-            multiply(y[b], w2_q[1], b, h_q[1], False, True)
-            results = keep.tile([P, S], F32, name="results%d" % b)
-            nc.scalar.copy(results[:], y[b][:])
-            nc.vector.tensor_tensor(windows[b][:].indirect(offsets[:]), results[:], gates[:, b, :], MULT)
+        for b in range(2):
+            finish(b, ya, FIRST)
+        copy_plain("u0", ((SC, 256, 512),))
+        for b in range(2):
+            multiply(yb[b], "u0", b, SECOND, "ha", True, False)
+            multiply(yb[b], "u1", b, SECOND, "hb", False, True)
+        quantize("u0", ((256, 512),))
+        finish(0, yb, SECOND)
+        nc.sync.dma_start(out=out[0:P, :], in_=windows[0][:])
+        copy_plain("u1", ((SC, 256, 512),))
+        finish(1, yb, SECOND)
+        nc.sync.dma_start(out=out[P : 2 * P, :], in_=windows[1][:])
+        quantize("u1", ((256, 512),))
+        for b in range(2, 4):
+            for y, tokens in ((ya, FIRST), (yb, SECOND)):
+                multiply(y[b], "u0", b, tokens, "ha", True, False)
+                multiply(y[b], "u1", b, tokens, "hb", False, True)
+                finish(b, y, tokens)
             nc.sync.dma_start(out=out[b * P : (b + 1) * P, :], in_=windows[b][:])

from contextlib import ExitStack

import concourse.mybir as mybir

K, T, S, H, N = 1536, 1024, 512, 1024, 512
FLOPS = 2 * S * H * (K + N)

F32 = mybir.dt.float32
BF16 = mybir.dt.bfloat16
U32 = mybir.dt.uint32
U16 = mybir.dt.uint16
U8 = mybir.dt.uint8
FP8X4 = mybir.dt.float8_e4m3fn_x4
MULT = mybir.AluOpType.mult
RELU = mybir.ActivationFunctionType.Relu
SQUARE = mybir.ActivationFunctionType.Square

P = 128
PASS = 512
HALF = 512


def tile_picked_place_mlp_relu2_srt_l_kernel(tc, xT, w1, w2, gate, offs, out):
    nc = tc.nc
    with ExitStack() as ctx:
        keep = ctx.enter_context(tc.tile_pool(name="keep", bufs=1))
        psum = ctx.enter_context(tc.psum_pool(name="psum", bufs=8))

        offsets = keep.tile([P, S // 16], U16, name="offsets")
        gates = [keep.tile([P, S], F32, name="gate%d" % b) for b in range(4)]
        windows = [keep.tile([P, T], F32, name="window%d" % b) for b in range(4)]
        raw = {}

        def load(name, rows):
            raw[name] = keep.tile([P, 4, rows.shape[1]], F32, name=name + "_raw")
            nc.sync.dma_start(out=raw[name][:], in_=rows.rearrange("(p j) w -> p j w", j=4))

        load("x0", xT[0:512, :])
        load("w0", w1[0:512, :])
        load("x1", xT[512:1024, :])
        load("a1", w1[512:1024, 0:512])
        load("x2", xT[1024:1536, :])
        load("a2", w1[1024:1536, 0:512])
        load("b1", w1[512:1024, 512:1024])
        load("b2", w1[1024:1536, 512:1024])
        load("u0", w2[0:512, :])
        load("u1", w2[512:1024, :])
        nc.sync.dma_start(offsets[:], offs)
        for b in range(4):
            nc.sync.dma_start(out=gates[b][:], in_=gate[b * P : (b + 1) * P, :])
        for b in range(4):
            nc.vector.memset(windows[b][:], 0.0)

        grouped = {}
        codes = {}

        def shares(v, total):
            return [s for s in ((nc.vector.tensor_copy, 0, v), (nc.scalar.copy, v, total)) if s[1] < s[2]]

        def copy_plain(name, pieces):
            src = raw[name]
            if name not in grouped:
                grouped[name] = keep.tile([P, 512, 4], BF16, name=name + "_grouped", align_bytes=64)
            for engine_copy, lo, hi in pieces:
                engine_copy(
                    out=grouped[name][:, lo:hi, :].rearrange("p (c i) j -> p c j i", i=4),
                    in_=src[:, :, lo:hi].rearrange("p j (c i) -> p c j i", i=4),
                )

        def copy_permuted(name, src, v):
            grouped[name] = keep.tile([P, 4, P, 4], BF16, name=name + "_grouped", align_bytes=64)
            for engine_copy, lo, hi in shares(v, P):
                engine_copy(
                    out=grouped[name][:, :, lo:hi, :].rearrange("p t m j -> p m j t"),
                    in_=src[:, :, 4 * lo : 4 * hi].rearrange("p j (m t) -> p m j t", t=4),
                )

        def quantize(name, parts=((0, 512),)):
            src = grouped[name]
            flat = src[:].rearrange("p t m j -> p (t m j)") if len(src.shape) == 4 else src[:].rearrange("p w j -> p (w j)")
            if name not in codes:
                codes[name] = (
                    keep.tile([P, 512], U32, name=name + "_codes", align_bytes=64),
                    keep.tile([P, 512], U8, name=name + "_scales", align_bytes=64),
                )
            words, scales = codes[name]
            for lo, hi in parts:
                nc.vector.quantize_mx(out=words[:, lo:hi].bitcast(FP8X4), scales=scales[:, lo:hi], in_=flat[:, 4 * lo : 4 * hi])

        QUARTERS = [(128 * t, 128 * t + 128) for t in range(4)]

        def multiply(acc, weights, t, tokens, moving, first, last):
            cols = slice(t * P, (t + 1) * P)
            nc.tensor.matmul_mx(
                out=acc[:],
                lhsT=codes[weights][0][:, cols].bitcast(FP8X4),
                lhsT_scale=codes[weights][1][:, cols],
                rhs=codes[moving][0][:, tokens].bitcast(FP8X4),
                rhs_scale=codes[moving][1][:, tokens],
                start=first,
                stop=last,
            )

        ALL = slice(0, S)
        acc = {}

        def layer1(half, c):
            if c == 0:
                acc[half] = [psum.tile([P, S], F32, name="bank") for t in range(4)]
            for t in range(4):
                multiply(acc[half][t], "%s%d" % (half, c), t, ALL, "x%d" % c, c == 0, c == 2)

        positive = {}

        def relu(half, engines):
            positive[half] = keep.tile([P, 4, S], F32, name=half + "_positive")
            for t in range(4):
                if engines[t] == "S":
                    nc.scalar.activation(positive[half][:, t, :], acc[half][t][:], RELU)
                else:
                    nc.vector.tensor_scalar_max(positive[half][:, t, :], acc[half][t][:], 0.0)

        def square(half, lo, mid, hi):
            name = "h" + half
            if name not in grouped:
                grouped[name] = keep.tile([P, S, 4], BF16, name=name + "_grouped", align_bytes=64)
            for on_scalar, a, b in ((False, lo, mid), (True, mid, hi)):
                if a == b:
                    continue
                dst = grouped[name][:, a:b, :].rearrange("p (c i) t -> p c t i", i=4)
                src = positive[half][:, :, a:b].rearrange("p t (c i) -> p c t i", i=4)
                if on_scalar:
                    nc.scalar.activation(dst, src, SQUARE)
                else:
                    nc.vector.tensor_tensor(dst, src, src, MULT)

        VC, SC = nc.vector.tensor_copy, nc.scalar.copy
        EVEN = ((VC, 0, 256), (SC, 256, 512))
        copy_plain("x0", EVEN)
        copy_permuted("a0", raw["w0"][:, :, 0:512], 80)
        quantize("x0")
        copy_permuted("b0", raw["w0"][:, :, 512:1024], 64)
        quantize("a0")
        layer1("a", 0)
        quantize("b0")
        copy_plain("x1", EVEN)
        quantize("x1")
        copy_permuted("a1", raw["a1"], 80)
        quantize("a1")
        layer1("a", 1)
        copy_plain("x2", EVEN)
        quantize("x2")
        copy_permuted("a2", raw["a2"], 80)
        quantize("a2", QUARTERS)
        layer1("a", 2)
        relu("a", "SVSV")
        copy_permuted("b1", raw["b1"], 96)
        square("a", 0, 192, 512)
        quantize("b1")
        layer1("b", 0)
        layer1("b", 1)
        quantize("ha")
        copy_permuted("b2", raw["b2"], 88)
        quantize("b2", QUARTERS)
        layer1("b", 2)
        copy_plain("u0", ((VC, 0, 256),))
        relu("b", "SVSV")
        quantize("u0", ((0, 256),))
        FIRST, SECOND = slice(0, 256), slice(256, 512)
        ya = [psum.tile([P, 256], F32, name="bank") for b in range(4)]
        for b in range(2):
            multiply(ya[b], "u0", b, FIRST, "ha", True, False)
        square("b", 0, 128, 256)
        quantize("hb", ((0, 256),))
        square("b", 256, 256, 512)
        copy_plain("u1", ((VC, 0, 256),))
        quantize("u1", ((0, 256),))
        for b in range(2):
            multiply(ya[b], "u1", b, FIRST, "hb", False, True)
        quantize("hb", ((256, 512),))
        yb = [psum.tile([P, 256], F32, name="bank") for b in range(4)]
        results = [keep.tile([P, S], F32, name="results%d" % b) for b in range(4)]

        def finish(b, y, tokens):
            lo, hi = tokens.start, tokens.stop
            nc.scalar.copy(results[b][:, lo:hi], y[b][:])
            nc.vector.tensor_tensor(
                windows[b][:].indirect(offsets[:, lo // 16 : hi // 16]), results[b][:, lo:hi], gates[b][:, lo:hi], MULT
            )

        for b in range(2):
            finish(b, ya, FIRST)
        copy_plain("u0", ((SC, 256, 512),))
        for b in range(2):
            multiply(yb[b], "u0", b, SECOND, "ha", True, False)
            multiply(yb[b], "u1", b, SECOND, "hb", False, True)
        quantize("u0", ((256, 512),))
        finish(0, yb, SECOND)
        nc.sync.dma_start(out=out[0:P, :], in_=windows[0][:])
        copy_plain("u1", ((SC, 256, 512),))
        finish(1, yb, SECOND)
        nc.sync.dma_start(out=out[P : 2 * P, :], in_=windows[1][:])
        quantize("u1", ((256, 512),))
        for b in range(2, 4):
            for y, tokens in ((ya, FIRST), (yb, SECOND)):
                multiply(y[b], "u0", b, tokens, "ha", True, False)
                multiply(y[b], "u1", b, tokens, "hb", False, True)
                finish(b, y, tokens)
            nc.sync.dma_start(out=out[b * P : (b + 1) * P, :], in_=windows[b][:])
